import numpy as np
CORES = [9,17,137,145,265,273,393,401]
N = 8
TIMES = 2
def setup_inputs(rng):
    x = (rng.standard_normal((N, 128, 128), dtype=np.float32) / np.float32(np.sqrt(512 * N)))
    return {"x": x, "xt": x.transpose(0, 2, 1).copy()}
def setup_inputs_big(rng):
    d = setup_inputs(rng)
    for k in ("x", "xt"): d[k] = (d[k].astype(np.float32) * 1024.0).astype(d[k].dtype)
    return d
def setup_inputs_small(rng):
    d = setup_inputs(rng)
    for k in ("x", "xt"): d[k] = (d[k].astype(np.float32) * (1 / 1024.0)).astype(d[k].dtype)
    return d
def setup_inputs_apart(rng):
    d = setup_inputs(rng)
    f = (10.0 ** rng.permutation(np.linspace(-1.5, 1.5, N))).astype(np.float32).reshape(N, 1, 1)
    for k in ("x", "xt"): d[k] = (d[k].astype(np.float32) * f).astype(d[k].dtype)
    return d
def reference(x, xt):
    X = list(x.astype(np.float64))
    for _ in range(TIMES):
        G = sum(a.T @ a for a in X)
        X = [1.5 * a - 0.5 * (a @ G) for a in X]
    return {"y": np.stack(X).astype(np.float32)}

@@ -1,0 +1,161 @@
+from concourse.bass import DstId, RemoteDMATransfer
+from concourse.mybir import AluOpType
+
+SIM_CORES = 512
+D = 128
+F32 = "float32"
+
+N_ON, N_OFF, N_HLP = 8, 8, 4
+
+_SB = ["xa", "xb", "xts", "half", "s", "rc", "rh", "rk", "h", "h225", "hb", "t", "b", "w", "x225", "ys"]
+_PS = ["pg", "pm1", "pm2", "pm3", "pv", "pc"]
+SCRATCH = {}
+for _n in _SB:
+    SCRATCH[_n] = ("sbuf", [D, D], F32)
+for _n in _PS:
+    SCRATCH[_n] = ("psum", [D, 4 * D], F32)
+
+SEMAPHORES = ["ldx", "ldxt", "st", "snt", "xa_in", "xb_in", "rc_in", "rh_in", "rk_in",
+              "c0", "c1", "mg", "m1", "m2", "m3",
+              "vx", "vs", "va0", "va1", "va2", "vh", "vh2", "vhb", "vt", "vb1", "vb", "vw", "vy"]
+
+
+def _take(mask, n, skip=0):
+    bits = [1 << i for i in range(mask.bit_length()) if (mask >> i) & 1]
+    out = 0
+    for b in bits[skip:skip + n]:
+        out |= b
+    return out
+
+
+def _plan(T, topo):
+    ranks = list(T.cores)
+    plan = {}
+    for r in ranks:
+        peer = [o for o in ranks if topo.same_plane(r, o)][0]
+        far = [o for o in ranks if topo.rack(topo.host(o)) != topo.rack(topo.host(r)) and topo.may_write(r, o)][0]
+        near = [o for o in ranks if o != r and topo.host(o) == topo.host(r)][0]
+        farx = [o for o in ranks if o != far and topo.host(o) == topo.host(far)][0]
+        cand = [c for c in range(SIM_CORES)
+                if topo.host(c) == topo.host(r) and topo.chip(c) == topo.chip(r) and c not in ranks
+                and topo.may_write(c, near) and topo.may_write(c, farx)]
+        cand.sort(key=lambda c: (topo.die(c) != topo.die(r), c))
+        plan[r] = dict(peer=peer, far=far, near=near, farx=farx, helper=cand[0])
+    return plan
+
+
+def _xfer(topo, src_core, dst_core, dst_ap, src_ap, sem, mask):
+    rid, pid = topo.addr(dst_core, src_core)
+    return RemoteDMATransfer(dst_ids=[DstId(rid=rid, pnc=pid)], dma_engine_mask=mask, remote_sem=sem,
+                             src=src_ap, dst=dst_ap)
+
+
+def _pair_sum(g, T, first_sem, first_n, n_xb):
+    s, te, ve = T.sem, g.tensor, g.vector
+    te.wait_ge(first_sem, first_n)
+    te.matmul(T.pg[:, 0:D], T.xa[:], T.xa[:], start=True, stop=False)
+    te.wait_ge(s.xb_in, n_xb)
+    te.matmul(T.pg[:, 0:D], T.xb[:], T.xb[:], start=False, stop=True).then_inc(s.mg, 1)
+    ve.wait_ge(s.c0, 1)
+    ve.wait_ge(s.mg, 1)
+    ve.tensor_tensor(T.s[:], T.pg[:, 0:D], T.half[:], AluOpType.mult).then_inc(s.vs, 1)
+
+
+def _helper_program(g, core, T, topo, p):
+    s = T.sem
+    g.vector.memset(T.half[:], 0.5).then_inc(s.c0, 1)
+    _pair_sum(g, T, s.xa_in, N_ON, N_OFF)
+    m = topo.mask(core, p["near"]) & topo.mask(core, p["farx"])
+    g.wait_ge(s.vs, 1)
+    g.remote_dma_fused([
+        _xfer(topo, core, p["farx"], T.rk[:], T.s[:], s.rk_in, _take(m, N_HLP)),
+        _xfer(topo, core, p["near"], T.rh[:], T.s[:], s.rh_in, _take(m, N_HLP, N_HLP)),
+    ], local_sem=s.snt)
+    g.wait_ge(s.snt, 2 * N_HLP)
+
+
+def _rank_program(g, core, T, topo, plan):
+    s, te, ve = T.sem, g.tensor, g.vector
+    p = plan[core]
+    add, sub, mul = AluOpType.add, AluOpType.subtract, AluOpType.mult
+    c225, c1078, c1687 = T.pc[:, 0:D], T.pc[:, D:2 * D], T.pc[:, 2 * D:3 * D]
+    a0, a1, a2, b1 = T.pv[:, 0:D], T.pv[:, D:2 * D], T.pv[:, 2 * D:3 * D], T.pv[:, 3 * D:4 * D]
+
+    g.sync.dma_start(T.xa[:], T.x[:]).then_inc(s.ldx, 16)
+    g.scalar.dma_start(T.xts[:], T.xt[:]).then_inc(s.ldxt, 16)
+
+    m_off = _take(topo.mask(core, p["peer"]), N_OFF)
+    m_on = _take(topo.mask(core, p["helper"]) & ~m_off, N_ON)
+    g.wait_ge(s.ldx, 16)
+    g.remote_dma_fused([
+        _xfer(topo, core, plan[p["peer"]]["helper"], T.xb[:], T.xa[:], s.xb_in, m_off),
+        _xfer(topo, core, p["helper"], T.xa[:], T.xa[:], s.xa_in, m_on),
+    ], local_sem=s.snt)
+    rid, pid = topo.addr(p["peer"], core)
+    g.remote_dma(T.xb[:], T.xa[:], s.xb_in, s.snt, pid, rid, m_off)
+
+    ve.memset(T.half[:], 0.5).then_inc(s.c0, 1)
+    ve.memset(c225, 2.25).then_inc(s.c1, 1)
+    ve.memset(c1078, 1.078125).then_inc(s.c1, 1)
+    ve.memset(c1687, 1.6875).then_inc(s.c1, 1)
+    ve.wait_ge(s.c1, 3)
+    ve.wait_ge(s.ldx, 16)
+    ve.tensor_tensor(T.x225[:], T.xa[:], c225, mul).then_inc(s.vx, 1)
+
+    _pair_sum(g, T, s.ldx, 16, N_OFF)
+
+    rid, pid = topo.addr(p["far"], core)
+    g.wait_ge(s.vs, 1)
+    g.remote_dma(T.rc[:], T.s[:], s.rc_in, s.snt, pid, rid, _take(topo.mask(core, p["far"]), N_OFF))
+
+    ve.tensor_tensor(a0, T.pg[:, 0:D], T.half[:], mul).then_inc(s.va0, 1)
+    ve.wait_ge(s.va0, 1)
+    ve.wait_ge(s.rc_in, N_OFF)
+    ve.tensor_tensor(a1, a0, T.rc[:], add).then_inc(s.va1, 1)
+    ve.wait_ge(s.va1, 1)
+    ve.wait_ge(s.rh_in, N_HLP)
+    ve.tensor_tensor(a2, a1, T.rh[:], add).then_inc(s.va2, 1)
+    ve.wait_ge(s.va2, 1)
+    ve.wait_ge(s.rk_in, N_HLP)
+    ve.tensor_tensor(T.h[:], a2, T.rk[:], add).then_inc(s.vh, 1)
+
+    te.wait_ge(s.vh, 1)
+    te.matmul(T.pm1[:, 0:D], T.h[:], T.h[:], start=True, stop=True).then_inc(s.m1, 1)
+    ve.wait_ge(s.vh, 1)
+    ve.tensor_tensor(T.h225[:], T.h[:], c225, mul).then_inc(s.vh2, 1)
+    ve.tensor_tensor(T.hb[:], T.h[:], c1078, mul).then_inc(s.vhb, 1)
+    ve.wait_ge(s.vh2, 1)
+    ve.wait_ge(s.m1, 1)
+    ve.tensor_tensor(T.t[:], T.pm1[:, 0:D], T.h225[:], sub).then_inc(s.vt, 1)
+
+    te.wait_ge(s.vt, 1)
+    te.matmul(T.pm2[:, 0:D], T.t[:], T.t[:], start=True, stop=True).then_inc(s.m2, 1)
+    ve.wait_ge(s.vt, 1)
+    ve.tensor_tensor(b1, T.t[:], c1687, mul).then_inc(s.vb1, 1)
+    ve.wait_ge(s.vb1, 1)
+    ve.wait_ge(s.vhb, 1)
+    ve.tensor_tensor(T.b[:], b1, T.hb[:], sub).then_inc(s.vb, 1)
+    ve.wait_ge(s.vb, 1)
+    ve.wait_ge(s.m2, 1)
+    ve.tensor_tensor(T.w[:], T.pm2[:, 0:D], T.b[:], add).then_inc(s.vw, 1)
+
+    te.wait_ge(s.vw, 1)
+    te.wait_ge(s.ldxt, 16)
+    te.matmul(T.pm3[:, 0:D], T.xts[:], T.w[:], start=True, stop=True).then_inc(s.m3, 1)
+    ve.wait_ge(s.vx, 1)
+    ve.wait_ge(s.m3, 1)
+    ve.tensor_tensor(T.ys[:], T.pm3[:, 0:D], T.x225[:], add).then_inc(s.vy, 1)
+    g.sync.wait_ge(s.vy, 1)
+    g.sync.dma_start(T.y[:], T.ys[:]).then_inc(s.st, 16)
+    g.sync.wait_ge(s.st, 16)
+    g.wait_ge(s.snt, N_ON + 3 * N_OFF)
+
+
+def rank_program(g, core, T, topo):
+    plan = _plan(T, topo)
+    if T.rank_of(core) is not None:
+        _rank_program(g, core, T, topo, plan)
+        return
+    for r in plan:
+        if plan[r]["helper"] == core:
+            _helper_program(g, core, T, topo, plan[r])

@@ -3,27 +3,35 @@ from concourse.mybir import AluOpType
 
 SIM_CORES = 512
 D = 128
+HF = D // 2
 F32 = "float32"
 
-N_ON, N_OFF, N_HLP = 8, 8, 4
+K = 2
+W = D // K
+N_OFF = 8
+N_BLK = 4
+N_HLP = 4
 
-_SB = ["xa", "xb", "xts", "half", "s", "rc", "rh", "rk", "h", "h225", "hb", "t", "b", "w", "x225", "ys"]
-_PS = ["pg", "pm1", "pm2", "pm3", "pv", "pc"]
-SCRATCH = {}
+_SB = ["xa", "xb", "xts", "half", "gs", "s", "rc", "rh", "rk", "h", "h225", "hb", "t", "b", "w", "x225", "ys"]
+_PS = ["pgo", "pg", "pm1", "pm2", "pm3", "pv", "pc"]
+SCRATCH = {"ga": ("sbuf", [D, W], F32), "gb": ("sbuf", [D, W], F32), "sb": ("sbuf", [D, W], F32)}
 for _n in _SB:
     SCRATCH[_n] = ("sbuf", [D, D], F32)
 for _n in _PS:
     SCRATCH[_n] = ("psum", [D, 4 * D], F32)
 
-SEMAPHORES = ["ldx", "ldxt", "st", "snt", "xa_in", "xb_in", "rc_in", "rh_in", "rk_in",
-              "c0", "c1", "mg", "m1", "m2", "m3",
-              "vx", "vs", "va0", "va1", "va2", "vh", "vh2", "vhb", "vt", "vb1", "vb", "vw", "vy"]
+SEMAPHORES = ["ldx", "ldxt", "st", "snt1", "snt", "ga_in", "gb_in", "xb_in", "rc_in", "rh_in", "rk_in",
+              "c0", "c1", "mgo", "mg", "m1", "m2", "m2b", "m3", "m3b",
+              "vgs", "vx", "vs", "va0", "va1", "va2", "vh", "vh2", "vhb", "vt", "vb1", "vb", "vw", "vwb", "vy", "vyb"]
+
+
+def _bits(mask):
+    return [1 << i for i in range(mask.bit_length()) if (mask >> i) & 1]
 
 
 def _take(mask, n, skip=0):
-    bits = [1 << i for i in range(mask.bit_length()) if (mask >> i) & 1]
     out = 0
-    for b in bits[skip:skip + n]:
+    for b in _bits(mask)[skip:skip + n]:
         out |= b
     return out
 
@@ -36,11 +44,12 @@ def _plan(T, topo):
         far = [o for o in ranks if topo.rack(topo.host(o)) != topo.rack(topo.host(r)) and topo.may_write(r, o)][0]
         near = [o for o in ranks if o != r and topo.host(o) == topo.host(r)][0]
         farx = [o for o in ranks if o != far and topo.host(o) == topo.host(far)][0]
-        cand = [c for c in range(SIM_CORES)
-                if topo.host(c) == topo.host(r) and topo.chip(c) == topo.chip(r) and c not in ranks
-                and topo.may_write(c, near) and topo.may_write(c, farx)]
-        cand.sort(key=lambda c: (topo.die(c) != topo.die(r), c))
-        plan[r] = dict(peer=peer, far=far, near=near, farx=farx, helper=cand[0])
+        own = [c for c in range(SIM_CORES)
+               if topo.host(c) == topo.host(r) and topo.chip(c) == topo.chip(r) and c not in ranks
+               and topo.may_write(c, near) and topo.may_write(c, farx)]
+        cand = sorted(own, key=lambda c: (len([o for o in own if o < c and topo.die(o) == topo.die(c)]),
+                                          topo.die(c) != topo.die(r)))
+        plan[r] = dict(peer=peer, far=far, near=near, farx=farx, helpers=cand[:K])
     return plan
 
 
@@ -50,26 +59,17 @@ def _xfer(topo, src_core, dst_core, dst_ap, src_ap, sem, mask):
                              src=src_ap, dst=dst_ap)
 
 
-def _pair_sum(g, T, first_sem, first_n, n_xb):
-    s, te, ve = T.sem, g.tensor, g.vector
-    te.wait_ge(first_sem, first_n)
-    te.matmul(T.pg[:, 0:D], T.xa[:], T.xa[:], start=True, stop=False)
-    te.wait_ge(s.xb_in, n_xb)
-    te.matmul(T.pg[:, 0:D], T.xb[:], T.xb[:], start=False, stop=True).then_inc(s.mg, 1)
-    ve.wait_ge(s.c0, 1)
-    ve.wait_ge(s.mg, 1)
-    ve.tensor_tensor(T.s[:], T.pg[:, 0:D], T.half[:], AluOpType.mult).then_inc(s.vs, 1)
-
-
-def _helper_program(g, core, T, topo, p):
+def _helper_program(g, core, T, topo, p, k):
     s = T.sem
-    g.vector.memset(T.half[:], 0.5).then_inc(s.c0, 1)
-    _pair_sum(g, T, s.xa_in, N_ON, N_OFF)
+    g.vector.wait_ge(s.ga_in, N_BLK)
+    g.vector.wait_ge(s.gb_in, N_BLK)
+    g.vector.tensor_tensor(T.sb[:], T.ga[:], T.gb[:], AluOpType.add).then_inc(s.vs, 1)
     m = topo.mask(core, p["near"]) & topo.mask(core, p["farx"])
+    c = slice(k * W, (k + 1) * W)
     g.wait_ge(s.vs, 1)
     g.remote_dma_fused([
-        _xfer(topo, core, p["farx"], T.rk[:], T.s[:], s.rk_in, _take(m, N_HLP)),
-        _xfer(topo, core, p["near"], T.rh[:], T.s[:], s.rh_in, _take(m, N_HLP, N_HLP)),
+        _xfer(topo, core, p["farx"], T.rk[:, c], T.sb[:], s.rk_in, _take(m, N_HLP)),
+        _xfer(topo, core, p["near"], T.rh[:, c], T.sb[:], s.rh_in, _take(m, N_HLP, N_HLP)),
     ], local_sem=s.snt)
     g.wait_ge(s.snt, 2 * N_HLP)
 
@@ -82,28 +82,42 @@ def _rank_program(g, core, T, topo, plan):
     a0, a1, a2, b1 = T.pv[:, 0:D], T.pv[:, D:2 * D], T.pv[:, 2 * D:3 * D], T.pv[:, 3 * D:4 * D]
 
     g.sync.dma_start(T.xa[:], T.x[:]).then_inc(s.ldx, 16)
-    g.scalar.dma_start(T.xts[:], T.xt[:]).then_inc(s.ldxt, 16)
 
-    m_off = _take(topo.mask(core, p["peer"]), N_OFF)
-    m_on = _take(topo.mask(core, p["helper"]) & ~m_off, N_ON)
-    g.wait_ge(s.ldx, 16)
-    g.remote_dma_fused([
-        _xfer(topo, core, plan[p["peer"]]["helper"], T.xb[:], T.xa[:], s.xb_in, m_off),
-        _xfer(topo, core, p["helper"], T.xa[:], T.xa[:], s.xa_in, m_on),
-    ], local_sem=s.snt)
+    m_off = topo.mask(core, p["peer"])
+    m_on = topo.mask(core, p["helpers"][0]) & ~m_off
     rid, pid = topo.addr(p["peer"], core)
-    g.remote_dma(T.xb[:], T.xa[:], s.xb_in, s.snt, pid, rid, m_off)
+    g.wait_ge(s.ldx, 16)
+    g.remote_dma(T.xb[:], T.xa[:], s.xb_in, s.snt1, pid, rid, _take(m_off, N_OFF))
+
+    te.wait_ge(s.ldx, 16)
+    te.matmul(T.pgo[:, 0:D], T.xa[:], T.xa[:], start=True, stop=True).then_inc(s.mgo, 1)
+    te.matmul(T.pg[:, 0:D], T.xa[:], T.xa[:], start=True, stop=False)
+    te.wait_ge(s.xb_in, N_OFF)
+    te.matmul(T.pg[:, 0:D], T.xb[:], T.xb[:], start=False, stop=True).then_inc(s.mg, 1)
 
     ve.memset(T.half[:], 0.5).then_inc(s.c0, 1)
     ve.memset(c225, 2.25).then_inc(s.c1, 1)
     ve.memset(c1078, 1.078125).then_inc(s.c1, 1)
     ve.memset(c1687, 1.6875).then_inc(s.c1, 1)
+    ve.wait_ge(s.c0, 1)
     ve.wait_ge(s.c1, 3)
-    ve.wait_ge(s.ldx, 16)
+    ve.wait_ge(s.mgo, 1)
+    ve.tensor_tensor(T.gs[:], T.pgo[:, 0:D], T.half[:], mul).then_inc(s.vgs, 1)
     ve.tensor_tensor(T.x225[:], T.xa[:], c225, mul).then_inc(s.vx, 1)
 
-    _pair_sum(g, T, s.ldx, 16, N_OFF)
+    xf = []
+    for k in range(K):
+        c = slice(k * W, (k + 1) * W)
+        xf.append(_xfer(topo, core, plan[p["peer"]]["helpers"][k], T.gb[:], T.gs[:, c], s.gb_in,
+                        _take(m_off, N_BLK, k * N_BLK)))
+        xf.append(_xfer(topo, core, p["helpers"][k], T.ga[:], T.gs[:, c], s.ga_in, _take(m_on, N_BLK, k * N_BLK)))
+    g.wait_ge(s.vgs, 1)
+    g.remote_dma_fused(xf, local_sem=s.snt1)
+    g.scalar.wait_ge(s.snt1, N_OFF + 2 * K * N_BLK)
+    g.scalar.dma_start(T.xts[:], T.xt[:]).then_inc(s.ldxt, 16)
 
+    ve.wait_ge(s.mg, 1)
+    ve.tensor_tensor(T.s[:], T.pg[:, 0:D], T.half[:], mul).then_inc(s.vs, 1)
     rid, pid = topo.addr(p["far"], core)
     g.wait_ge(s.vs, 1)
     g.remote_dma(T.rc[:], T.s[:], s.rc_in, s.snt, pid, rid, _take(topo.mask(core, p["far"]), N_OFF))
@@ -113,10 +127,10 @@ def _rank_program(g, core, T, topo, plan):
     ve.wait_ge(s.rc_in, N_OFF)
     ve.tensor_tensor(a1, a0, T.rc[:], add).then_inc(s.va1, 1)
     ve.wait_ge(s.va1, 1)
-    ve.wait_ge(s.rh_in, N_HLP)
+    ve.wait_ge(s.rh_in, K * N_HLP)
     ve.tensor_tensor(a2, a1, T.rh[:], add).then_inc(s.va2, 1)
     ve.wait_ge(s.va2, 1)
-    ve.wait_ge(s.rk_in, N_HLP)
+    ve.wait_ge(s.rk_in, K * N_HLP)
     ve.tensor_tensor(T.h[:], a2, T.rk[:], add).then_inc(s.vh, 1)
 
     te.wait_ge(s.vh, 1)
@@ -129,7 +143,9 @@ def _rank_program(g, core, T, topo, plan):
     ve.tensor_tensor(T.t[:], T.pm1[:, 0:D], T.h225[:], sub).then_inc(s.vt, 1)
 
     te.wait_ge(s.vt, 1)
-    te.matmul(T.pm2[:, 0:D], T.t[:], T.t[:], start=True, stop=True).then_inc(s.m2, 1)
+    te.wait_ge(s.vgs, 1)
+    te.matmul(T.pm2[:, 0:HF], T.t[:], T.t[:, 0:HF], start=True, stop=True).then_inc(s.m2, 1)
+    te.matmul(T.pgo[:, 0:HF], T.t[:], T.t[:, HF:D], start=True, stop=True).then_inc(s.m2b, 1)
     ve.wait_ge(s.vt, 1)
     ve.tensor_tensor(b1, T.t[:], c1687, mul).then_inc(s.vb1, 1)
     ve.wait_ge(s.vb1, 1)
@@ -137,18 +153,27 @@ def _rank_program(g, core, T, topo, plan):
     ve.tensor_tensor(T.b[:], b1, T.hb[:], sub).then_inc(s.vb, 1)
     ve.wait_ge(s.vb, 1)
     ve.wait_ge(s.m2, 1)
-    ve.tensor_tensor(T.w[:], T.pm2[:, 0:D], T.b[:], add).then_inc(s.vw, 1)
+    ve.tensor_tensor(T.w[:, 0:HF], T.pm2[:, 0:HF], T.b[:, 0:HF], add).then_inc(s.vw, 1)
+    ve.wait_ge(s.m2b, 1)
+    ve.tensor_tensor(T.w[:, HF:D], T.pgo[:, 0:HF], T.b[:, HF:D], add).then_inc(s.vwb, 1)
 
     te.wait_ge(s.vw, 1)
     te.wait_ge(s.ldxt, 16)
-    te.matmul(T.pm3[:, 0:D], T.xts[:], T.w[:], start=True, stop=True).then_inc(s.m3, 1)
+    te.matmul(T.pm3[:, 0:HF], T.xts[:], T.w[:, 0:HF], start=True, stop=True).then_inc(s.m3, 1)
+    te.wait_ge(s.vwb, 1)
+    te.wait_ge(s.vs, 1)
+    te.wait_ge(s.va0, 1)
+    te.matmul(T.pg[:, 0:HF], T.xts[:], T.w[:, HF:D], start=True, stop=True).then_inc(s.m3b, 1)
     ve.wait_ge(s.vx, 1)
     ve.wait_ge(s.m3, 1)
-    ve.tensor_tensor(T.ys[:], T.pm3[:, 0:D], T.x225[:], add).then_inc(s.vy, 1)
+    ve.tensor_tensor(T.ys[:, 0:HF], T.pm3[:, 0:HF], T.x225[:, 0:HF], add).then_inc(s.vy, 1)
+    ve.wait_ge(s.m3b, 1)
+    ve.tensor_tensor(T.ys[:, HF:D], T.pg[:, 0:HF], T.x225[:, HF:D], add).then_inc(s.vyb, 1)
     g.sync.wait_ge(s.vy, 1)
+    g.sync.wait_ge(s.vyb, 1)
     g.sync.dma_start(T.y[:], T.ys[:]).then_inc(s.st, 16)
     g.sync.wait_ge(s.st, 16)
-    g.wait_ge(s.snt, N_ON + 3 * N_OFF)
+    g.wait_ge(s.snt, N_OFF)
 
 
 def rank_program(g, core, T, topo):
@@ -157,5 +182,5 @@ def rank_program(g, core, T, topo):
         _rank_program(g, core, T, topo, plan)
         return
     for r in plan:
-        if plan[r]["helper"] == core:
-            _helper_program(g, core, T, topo, plan[r])
+        if core in plan[r]["helpers"]:
+            _helper_program(g, core, T, topo, plan[r], plan[r]["helpers"].index(core))

from concourse.bass import DstId, RemoteDMATransfer
from concourse.mybir import AluOpType

SIM_CORES = 512
D = 128
HF = D // 2
F32 = "float32"

K = 2
W = D // K
N_OFF = 8
N_BLK = 4
N_HLP = 4

_SB = ["xa", "xb", "xts", "half", "gs", "s", "rc", "rh", "rk", "h", "h225", "hb", "t", "b", "w", "x225", "ys"]
_PS = ["pgo", "pg", "pm1", "pm2", "pm3", "pv", "pc"]
SCRATCH = {"ga": ("sbuf", [D, W], F32), "gb": ("sbuf", [D, W], F32), "sb": ("sbuf", [D, W], F32)}
for _n in _SB:
    SCRATCH[_n] = ("sbuf", [D, D], F32)
for _n in _PS:
    SCRATCH[_n] = ("psum", [D, 4 * D], F32)

SEMAPHORES = ["ldx", "ldxt", "st", "snt1", "snt", "ga_in", "gb_in", "xb_in", "rc_in", "rh_in", "rk_in",
              "c0", "c1", "mgo", "mg", "m1", "m2", "m2b", "m3", "m3b",
              "vgs", "vx", "vs", "va0", "va1", "va2", "vh", "vh2", "vhb", "vt", "vb1", "vb", "vw", "vwb", "vy", "vyb"]


def _bits(mask):
    return [1 << i for i in range(mask.bit_length()) if (mask >> i) & 1]


def _take(mask, n, skip=0):
    out = 0
    for b in _bits(mask)[skip:skip + n]:
        out |= b
    return out


def _plan(T, topo):
    ranks = list(T.cores)
    plan = {}
    for r in ranks:
        peer = [o for o in ranks if topo.same_plane(r, o)][0]
        far = [o for o in ranks if topo.rack(topo.host(o)) != topo.rack(topo.host(r)) and topo.may_write(r, o)][0]
        near = [o for o in ranks if o != r and topo.host(o) == topo.host(r)][0]
        farx = [o for o in ranks if o != far and topo.host(o) == topo.host(far)][0]
        own = [c for c in range(SIM_CORES)
               if topo.host(c) == topo.host(r) and topo.chip(c) == topo.chip(r) and c not in ranks
               and topo.may_write(c, near) and topo.may_write(c, farx)]
        cand = sorted(own, key=lambda c: (len([o for o in own if o < c and topo.die(o) == topo.die(c)]),
                                          topo.die(c) != topo.die(r)))
        plan[r] = dict(peer=peer, far=far, near=near, farx=farx, helpers=cand[:K])
    return plan


def _xfer(topo, src_core, dst_core, dst_ap, src_ap, sem, mask):
    rid, pid = topo.addr(dst_core, src_core)
    return RemoteDMATransfer(dst_ids=[DstId(rid=rid, pnc=pid)], dma_engine_mask=mask, remote_sem=sem,
                             src=src_ap, dst=dst_ap)


def _helper_program(g, core, T, topo, p, k):
    s = T.sem
    g.vector.wait_ge(s.ga_in, N_BLK)
    g.vector.wait_ge(s.gb_in, N_BLK)
    g.vector.tensor_tensor(T.sb[:], T.ga[:], T.gb[:], AluOpType.add).then_inc(s.vs, 1)
    m = topo.mask(core, p["near"]) & topo.mask(core, p["farx"])
    c = slice(k * W, (k + 1) * W)
    g.wait_ge(s.vs, 1)
    g.remote_dma_fused([
        _xfer(topo, core, p["farx"], T.rk[:, c], T.sb[:], s.rk_in, _take(m, N_HLP)),
        _xfer(topo, core, p["near"], T.rh[:, c], T.sb[:], s.rh_in, _take(m, N_HLP, N_HLP)),
    ], local_sem=s.snt)
    g.wait_ge(s.snt, 2 * N_HLP)


def _rank_program(g, core, T, topo, plan):
    s, te, ve = T.sem, g.tensor, g.vector
    p = plan[core]
    add, sub, mul = AluOpType.add, AluOpType.subtract, AluOpType.mult
    c225, c1078, c1687 = T.pc[:, 0:D], T.pc[:, D:2 * D], T.pc[:, 2 * D:3 * D]
    a0, a1, a2, b1 = T.pv[:, 0:D], T.pv[:, D:2 * D], T.pv[:, 2 * D:3 * D], T.pv[:, 3 * D:4 * D]

    g.sync.dma_start(T.xa[:], T.x[:]).then_inc(s.ldx, 16)

    m_off = topo.mask(core, p["peer"])
    m_on = topo.mask(core, p["helpers"][0]) & ~m_off
    rid, pid = topo.addr(p["peer"], core)
    g.wait_ge(s.ldx, 16)
    g.remote_dma(T.xb[:], T.xa[:], s.xb_in, s.snt1, pid, rid, _take(m_off, N_OFF))

    te.wait_ge(s.ldx, 16)
    te.matmul(T.pgo[:, 0:D], T.xa[:], T.xa[:], start=True, stop=True).then_inc(s.mgo, 1)
    te.matmul(T.pg[:, 0:D], T.xa[:], T.xa[:], start=True, stop=False)
    te.wait_ge(s.xb_in, N_OFF)
    te.matmul(T.pg[:, 0:D], T.xb[:], T.xb[:], start=False, stop=True).then_inc(s.mg, 1)

    ve.memset(T.half[:], 0.5).then_inc(s.c0, 1)
    ve.memset(c225, 2.25).then_inc(s.c1, 1)
    ve.memset(c1078, 1.078125).then_inc(s.c1, 1)
    ve.memset(c1687, 1.6875).then_inc(s.c1, 1)
    ve.wait_ge(s.c0, 1)
    ve.wait_ge(s.c1, 3)
    ve.wait_ge(s.mgo, 1)
    ve.tensor_tensor(T.gs[:], T.pgo[:, 0:D], T.half[:], mul).then_inc(s.vgs, 1)
    ve.tensor_tensor(T.x225[:], T.xa[:], c225, mul).then_inc(s.vx, 1)

    xf = []
    for k in range(K):
        c = slice(k * W, (k + 1) * W)
        xf.append(_xfer(topo, core, plan[p["peer"]]["helpers"][k], T.gb[:], T.gs[:, c], s.gb_in,
                        _take(m_off, N_BLK, k * N_BLK)))
        xf.append(_xfer(topo, core, p["helpers"][k], T.ga[:], T.gs[:, c], s.ga_in, _take(m_on, N_BLK, k * N_BLK)))
    g.wait_ge(s.vgs, 1)
    g.remote_dma_fused(xf, local_sem=s.snt1)
    g.scalar.wait_ge(s.snt1, N_OFF + 2 * K * N_BLK)
    g.scalar.dma_start(T.xts[:], T.xt[:]).then_inc(s.ldxt, 16)

    ve.wait_ge(s.mg, 1)
    ve.tensor_tensor(T.s[:], T.pg[:, 0:D], T.half[:], mul).then_inc(s.vs, 1)
    rid, pid = topo.addr(p["far"], core)
    g.wait_ge(s.vs, 1)
    g.remote_dma(T.rc[:], T.s[:], s.rc_in, s.snt, pid, rid, _take(topo.mask(core, p["far"]), N_OFF))

    ve.tensor_tensor(a0, T.pg[:, 0:D], T.half[:], mul).then_inc(s.va0, 1)
    ve.wait_ge(s.va0, 1)
    ve.wait_ge(s.rc_in, N_OFF)
    ve.tensor_tensor(a1, a0, T.rc[:], add).then_inc(s.va1, 1)
    ve.wait_ge(s.va1, 1)
    ve.wait_ge(s.rh_in, K * N_HLP)
    ve.tensor_tensor(a2, a1, T.rh[:], add).then_inc(s.va2, 1)
    ve.wait_ge(s.va2, 1)
    ve.wait_ge(s.rk_in, K * N_HLP)
    ve.tensor_tensor(T.h[:], a2, T.rk[:], add).then_inc(s.vh, 1)

    te.wait_ge(s.vh, 1)
    te.matmul(T.pm1[:, 0:D], T.h[:], T.h[:], start=True, stop=True).then_inc(s.m1, 1)
    ve.wait_ge(s.vh, 1)
    ve.tensor_tensor(T.h225[:], T.h[:], c225, mul).then_inc(s.vh2, 1)
    ve.tensor_tensor(T.hb[:], T.h[:], c1078, mul).then_inc(s.vhb, 1)
    ve.wait_ge(s.vh2, 1)
    ve.wait_ge(s.m1, 1)
    ve.tensor_tensor(T.t[:], T.pm1[:, 0:D], T.h225[:], sub).then_inc(s.vt, 1)

    te.wait_ge(s.vt, 1)
    te.wait_ge(s.vgs, 1)
    te.matmul(T.pm2[:, 0:HF], T.t[:], T.t[:, 0:HF], start=True, stop=True).then_inc(s.m2, 1)
    te.matmul(T.pgo[:, 0:HF], T.t[:], T.t[:, HF:D], start=True, stop=True).then_inc(s.m2b, 1)
    ve.wait_ge(s.vt, 1)
    ve.tensor_tensor(b1, T.t[:], c1687, mul).then_inc(s.vb1, 1)
    ve.wait_ge(s.vb1, 1)
    ve.wait_ge(s.vhb, 1)
    ve.tensor_tensor(T.b[:], b1, T.hb[:], sub).then_inc(s.vb, 1)
    ve.wait_ge(s.vb, 1)
    ve.wait_ge(s.m2, 1)
    ve.tensor_tensor(T.w[:, 0:HF], T.pm2[:, 0:HF], T.b[:, 0:HF], add).then_inc(s.vw, 1)
    ve.wait_ge(s.m2b, 1)
    ve.tensor_tensor(T.w[:, HF:D], T.pgo[:, 0:HF], T.b[:, HF:D], add).then_inc(s.vwb, 1)

    te.wait_ge(s.vw, 1)
    te.wait_ge(s.ldxt, 16)
    te.matmul(T.pm3[:, 0:HF], T.xts[:], T.w[:, 0:HF], start=True, stop=True).then_inc(s.m3, 1)
    te.wait_ge(s.vwb, 1)
    te.wait_ge(s.vs, 1)
    te.wait_ge(s.va0, 1)
    te.matmul(T.pg[:, 0:HF], T.xts[:], T.w[:, HF:D], start=True, stop=True).then_inc(s.m3b, 1)
    ve.wait_ge(s.vx, 1)
    ve.wait_ge(s.m3, 1)
    ve.tensor_tensor(T.ys[:, 0:HF], T.pm3[:, 0:HF], T.x225[:, 0:HF], add).then_inc(s.vy, 1)
    ve.wait_ge(s.m3b, 1)
    ve.tensor_tensor(T.ys[:, HF:D], T.pg[:, 0:HF], T.x225[:, HF:D], add).then_inc(s.vyb, 1)
    g.sync.wait_ge(s.vy, 1)
    g.sync.wait_ge(s.vyb, 1)
    g.sync.dma_start(T.y[:], T.ys[:]).then_inc(s.st, 16)
    g.sync.wait_ge(s.st, 16)
    g.wait_ge(s.snt, N_OFF)


def rank_program(g, core, T, topo):
    plan = _plan(T, topo)
    if T.rank_of(core) is not None:
        _rank_program(g, core, T, topo, plan)
        return
    for r in plan:
        if core in plan[r]["helpers"]:
            _helper_program(g, core, T, topo, plan[r], plan[r]["helpers"].index(core))
